import numpy as np
import ml_dtypes


def mxq(x, axis, fmt="e4m3"):
    dtype, down = {"e4m3": (ml_dtypes.float8_e4m3fn, 7), "e5m2": (ml_dtypes.float8_e5m2, 14)}[fmt]
    v = np.moveaxis(np.asarray(x, np.float32).astype(ml_dtypes.bfloat16).astype(np.float64), axis, -1)
    blocks = v.reshape(v.shape[:-1] + (-1, 32))
    amax = np.abs(blocks).max(-1, keepdims=True)
    byte = np.maximum(np.where(amax > 0, np.frexp(amax)[1] - 1 + 127, 0) - down, 1)
    scale = np.exp2(byte - 127.0)
    codes = (blocks / scale).astype(np.float32).astype(dtype).astype(np.float64)
    return np.moveaxis((codes * scale).reshape(v.shape), -1, axis)


WIDE = False


def mx_kscale(k):
    if not WIDE:
        return np.ones(k)
    levels = np.array([10, -10, 5, -5, 0])
    if k % 512:
        return np.exp2(np.random.permutation(np.resize(levels, k // 32))).repeat(32)
    a = np.empty((k // 512, 16))
    for p in range(k // 512):
        a[p, :8] = np.random.permutation(np.resize(levels, 8))
        for g in range(8):
            far = levels[np.abs(levels - a[p, g]) >= 10]
            a[p, g + 8] = far[np.random.randint(len(far))]
    return np.exp2(a.ravel()).repeat(32)


def f64(x):
    return np.asarray(x).astype(np.float64)


def striped(idx):
    return np.tile(idx.reshape(-1, 16).T, (8, 1)).astype(np.uint16)


def unstriped(offs):
    return offs[:16].T.reshape(-1).astype(np.int64)


def striped8(idx):
    return np.concatenate([x.reshape(-1, 16).T for x in idx]).astype(np.uint16)


def runs(offs, k):
    lists = np.stack([offs[16 * r : 16 * r + 16].T.reshape(-1) for r in range(8)]).astype(np.int64)
    return lists[np.arange(k) % 512 // 64]


def pack_weight(w):
    k, n = w.shape
    w = f64(np.asarray(w, np.float32).astype(ml_dtypes.bfloat16)).reshape(k // 32, 32, n)
    amax = np.abs(w).max(1)
    byte = np.clip(np.where(amax > 0, np.frexp(amax)[1] - 1 + 127 - 7, 1), 1, 254)
    scaled = (w * np.exp2(127.0 - byte)[:, None, :]).reshape(k, n).astype(np.float32)
    words = np.ascontiguousarray(scaled.reshape(k // 512, 128, 4, n).transpose(0, 1, 3, 2)).astype(ml_dtypes.float8_e4m3fn).view(np.uint8)
    return words, np.ascontiguousarray(byte.astype(np.uint8).reshape(k // 512, 16, n))


def unpack_weight(words, scales):
    g, p, n, _ = words.shape
    vals = np.ascontiguousarray(words).view(ml_dtypes.float8_e4m3fn).astype(np.float64) * np.repeat(np.exp2(scales.astype(np.float64) - 127.0), 8, axis=1)[..., None]
    return vals.transpose(0, 1, 3, 2).reshape(g * 512, n)


K, T, S, H, W, C = 512, 2048, 512, 512, 256, 512


def setup_inputs():
    n = np.random.standard_normal
    s = mx_kscale(K)[:, None]
    packed_xT = pack_weight(n((K, T)) * s)
    perm = np.stack([np.random.permutation(S) for _ in range(8)])
    return {
        "x_words": packed_xT[0],
        "x_scales": packed_xT[1],
        "w1": (n((K, H)) / np.sqrt(K) / s).astype(np.float32),
        "gs": (np.random.uniform(0.5, 1.5, (K, 1)) / s).astype(np.float32),
        "offs": striped(np.random.permutation(T)[:S]),
        "n1": striped8(perm[:, :W]),
        "n2": striped8(perm[:, W:]),
        "n3": striped8(np.stack([np.random.permutation(S) for _ in range(8)])),
        "ca": striped(np.random.permutation(T)[:C]),
        "cb": striped(np.random.permutation(T)[:C]),
        "n4": striped8(np.stack([np.random.permutation(S) for _ in range(8)])),
        "n5": striped8(np.stack([np.random.permutation(S) for _ in range(8)])),
        "n6": striped8(np.stack([np.random.permutation(S) for _ in range(8)])),
        "n7": striped8(np.stack([np.random.permutation(S) for _ in range(8)])),
    }


def reference(x_words, x_scales, w1, gs, offs, n1, n2, n3, ca, cb, n4, n5, n6, n7):
    x_ca = unpack_weight(x_words, x_scales)[:, unstriped(ca)]
    xq = unpack_weight(x_words, x_scales)[:, unstriped(offs)]
    y = mxq(f64(w1), 0, "e4m3").T @ xq
    pa = y[np.arange(H)[:, None], runs(n1, H)]
    pb = y[np.arange(H)[:, None], runs(n2, H)]
    ra = pa - (0.5 * pb)
    ds = y.copy()
    ds[np.arange(H)[:, None], runs(n2, H)] = ra
    z = f64(gs) * (ds - (0.5 * (ds[np.arange(H)[:, None], runs(n3, H)])))
    zq = mxq(z, 0, "e4m3")
    a = 0.0625 * (x_ca.T @ zq)
    x_cb = unpack_weight(x_words, x_scales)[:, unstriped(cb)]
    b = 0.0625 * (x_cb.T @ zq)
    return np.maximum(a[np.arange(C)[:, None], runs(n4, C)] + b[np.arange(C)[:, None], runs(n6, C)], a[np.arange(C)[:, None], runs(n5, C)] + b[np.arange(C)[:, None], runs(n7, C)])

@@ -1,0 +1,170 @@
+from contextlib import ExitStack
+
+import concourse.mybir as mybir
+
+K, T, S, H, W, C = 512, 2048, 512, 512, 256, 512
+FLOPS = 2 * K * H * S + 2 * 2 * K * C * S
+
+F32 = mybir.dt.float32
+BF16 = mybir.dt.bfloat16
+I32 = mybir.dt.int32
+U32 = mybir.dt.uint32
+U16 = mybir.dt.uint16
+U8 = mybir.dt.uint8
+FP8X4 = mybir.dt.float8_e4m3fn_x4
+COPY = mybir.ActivationFunctionType.Copy
+ADD = mybir.AluOpType.add
+MULT = mybir.AluOpType.mult
+MAX = mybir.AluOpType.max
+
+P = 128
+PACK = 4
+Z_CHUNKS = ((0, 256), (256, 128), (384, 128))
+
+
+def tile_picked_ccmppathbfoldd_none_p_kernel(tc, x_words, x_scales, w1, gs, offs, n1, n2, n3, ca, cb, n4, n5, n6, n7, out):
+    nc = tc.nc
+    with ExitStack() as ctx:
+        lists = ctx.enter_context(tc.tile_pool(name="lists", bufs=1))
+        keep = ctx.enter_context(tc.tile_pool(name="keep", bufs=1))
+        work = ctx.enter_context(tc.tile_pool(name="work", bufs=2))
+        psum = ctx.enter_context(tc.psum_pool(name="psum", bufs=1))
+
+        def load_list(name, src):
+            tile = lists.tile(list(src.shape), U16, name=name)
+            nc.sync.dma_start(tile[:], src)
+            return tile
+
+        xs = keep.tile([P, T], U8, name="xs", align_bytes=64)
+        nc.vector.memset(xs[:].bitcast(I32), 0)
+        for q in range(4):
+            nc.sync.dma_start(xs[32 * q : 32 * q + 4, :].bitcast(I32), x_scales[0, 4 * q : 4 * q + 4, :].bitcast(I32))
+        offs_t = load_list("offs_t", offs)
+        w_rows = w1.rearrange("(p j) c -> p j c", j=PACK)
+        w_raw = []
+        for half in range(2):
+            raw = keep.tile([P, PACK, H // 2], F32, name="w_raw%d" % half)
+            nc.sync.dma_start(raw[:], w_rows[:, :, half * (H // 2) : (half + 1) * (H // 2)])
+            w_raw.append(raw)
+        xw = keep.tile([P, T], U32, name="xw", align_bytes=64)
+        nc.sync.dma_start(xw[:].bitcast(I32), x_words[0].rearrange("p n t -> p (n t)").bitcast(I32))
+        ca_t = load_list("ca_t", ca)
+        cb_t = load_list("cb_t", cb)
+        gs_t = keep.tile([P, PACK], F32, name="gs_t")
+        nc.sync.dma_start(gs_t[:], gs.rearrange("(p t) o -> p (t o)", t=PACK))
+        n1_t = load_list("n1_t", n1)
+        n2_t = load_list("n2_t", n2)
+        n3_t = load_list("n3_t", n3)
+        n4_t = load_list("n4_t", n4)
+        n5_t = load_list("n5_t", n5)
+        n6_t = load_list("n6_t", n6)
+        n7_t = load_list("n7_t", n7)
+
+        a_win = [keep.tile([P, 2 * S], F32, name="a_win%d" % t) for t in range(2)]
+        b_win = [keep.tile([P, 2 * S], F32, name="b_win%d" % t) for t in range(2)]
+        for win in a_win + b_win:
+            nc.vector.memset(win[:, S:], 0.0)
+
+        def gather_bytes(name, lst):
+            tile = keep.tile([P, S], U8, name=name, align_bytes=64)
+            nc.vector.tensor_copy(tile[:], xs[:].indirect(lst[:]))
+            return tile
+
+        def deal_bytes(name, plain):
+            tile = keep.tile([P, S], U8, name=name, align_bytes=64)
+            nc.vector.tensor_copy(
+                tile[:].bitcast(I32).rearrange("p (t g r) -> p t g r", t=PACK, r=2),
+                plain[:].bitcast(I32).rearrange("p (g t r) -> p t g r", t=PACK, r=2),
+            )
+            return tile
+
+        def gather_dealt_words(tile, lst):
+            nc.vector.tensor_copy(tile[:].rearrange("p (t g r) -> p g t r", t=PACK, r=8), xw[:].indirect(lst[:]))
+
+        xq_s = gather_bytes("xq_s", offs_t)
+        ca_s = deal_bytes("ca_s", gather_bytes("ca_plain", ca_t))
+
+        w_bf = keep.tile([P, PACK, P, PACK], BF16, name="w_bf", align_bytes=64)
+        for half in range(2):
+            nc.scalar.copy(
+                w_bf[:, :, half * 64 : (half + 1) * 64, :].rearrange("p t m j -> p m t j"),
+                w_raw[half][:].rearrange("p j (m t) -> p m t j", t=PACK),
+            )
+        w_q = keep.tile([P, H], U32, name="w_q", align_bytes=64)
+        w_s = keep.tile([P, H], U8, name="w_s", align_bytes=64)
+        nc.vector.quantize_mx(out=w_q[:].bitcast(FP8X4), scales=w_s[:], in_=w_bf[:].rearrange("p t m j -> p (t m j)"))
+
+        xq_w = keep.tile([P, S], U32, name="xq_w", align_bytes=64)
+        nc.vector.tensor_copy(xq_w[:], xw[:].indirect(offs_t[:]))
+
+        banks = [psum.tile([P, S], F32, name="bank%d" % i) for i in range(8)]
+        ds = []
+        for t in range(PACK):
+            cols = slice(t * P, (t + 1) * P)
+            nc.tensor.matmul_mx(banks[t][:], lhsT=w_q[:, cols].bitcast(FP8X4), lhsT_scale=w_s[:, cols],
+                                rhs=xq_w[:].bitcast(FP8X4), rhs_scale=xq_s[:], start=True, stop=True)
+            y = keep.tile([P, S], F32, name="ds%d" % t)
+            nc.scalar.activation(y[:], banks[t][:], COPY, scale=gs_t[:, t : t + 1])
+            ds.append(y)
+
+        ca_w = keep.tile([P, C], U32, name="ca_w", align_bytes=64)
+        gather_dealt_words(ca_w, ca_t)
+
+        halves = []
+        pa = []
+        pb = []
+        for t in range(PACK + 1):
+            if t < PACK:
+                first = keep.tile([P, W], F32, name="pa%d" % t)
+                nc.vector.tensor_copy(first[:], ds[t][:].indirect(n1_t[:]))
+                second = keep.tile([P, W], F32, name="pb%d" % t)
+                nc.vector.tensor_scalar(second[:], ds[t][:].indirect(n2_t[:]), -0.5, 0.0, MULT, ADD)
+                pa.append(first)
+                pb.append(second)
+            if t > 0:
+                u = t - 1
+                nc.vector.tensor_tensor(ds[u][:].indirect(n2_t[:]), pa[u][:], pb[u][:], ADD)
+                half_ds = keep.tile([P, S], F32, name="half_ds%d" % u, tag="half_ds%d" % u, align_bytes=64)
+                nc.scalar.activation(half_ds[:], ds[u][:], COPY, scale=-0.5)
+                halves.append(half_ds)
+
+        z_q = keep.tile([P, S], U32, name="z_q", align_bytes=64)
+        z_s = keep.tile([P, S], U8, name="z_s", align_bytes=64)
+        z_bf = []
+        for i, (c0, width) in enumerate(Z_CHUNKS):
+            zf = keep.tile([P, PACK, width], F32, name="zf%d" % i)
+            for t in range(PACK):
+                nc.vector.tensor_tensor(zf[:, t, :], halves[t][:].indirect(n3_t[:, c0 // 16 : (c0 + width) // 16]),
+                                        ds[t][:, c0 : c0 + width], ADD)
+            zb = keep.tile([P, width, PACK], BF16, name="zb%d" % i, tag="zb%d" % i, align_bytes=64)
+            nc.scalar.copy(zb[:], zf[:].rearrange("p t c -> p c t"))
+            z_bf.append(zb)
+            if i == len(Z_CHUNKS) - 1:
+                cb_w = keep.tile([P, C], U32, name="cb_w", tag="half_ds3", align_bytes=64)
+                gather_dealt_words(cb_w, cb_t)
+            for j in ([i - 1] if i > 0 else []) + ([i] if i == len(Z_CHUNKS) - 1 else []):
+                d0, dw = Z_CHUNKS[j]
+                nc.vector.quantize_mx(out=z_q[:, d0 : d0 + dw].bitcast(FP8X4), scales=z_s[:, d0 : d0 + dw],
+                                      in_=z_bf[j][:].rearrange("p c t -> p (c t)"))
+        cb_plain = keep.tile([P, S], U8, name="cb_plain", tag="zb2", align_bytes=64)
+        nc.vector.tensor_copy(cb_plain[:], xs[:].indirect(cb_t[:]))
+        cb_s = deal_bytes("cb_s", cb_plain)
+
+        out_rows = out.rearrange("(g t r) j -> t g r j", t=PACK, r=8)
+        for t in range(PACK):
+            cols = slice(t * P, (t + 1) * P)
+            for words, scales, win, bank in ((ca_w, ca_s, a_win[t % 2], banks[2 * t]), (cb_w, cb_s, b_win[t % 2], banks[2 * t + 1])):
+                nc.tensor.matmul_mx(bank[:], lhsT=words[:, cols].bitcast(FP8X4), lhsT_scale=scales[:, cols],
+                                    rhs=z_q[:].bitcast(FP8X4), rhs_scale=z_s[:], start=True, stop=True)
+                nc.scalar.activation(win[:, :S], bank[:], COPY, scale=0.0625)
+            a4 = work.tile([P, S], F32, name="a4")
+            nc.vector.tensor_copy(a4[:], a_win[t % 2][:].indirect(n4_t[:]))
+            a5 = work.tile([P, S], F32, name="a5")
+            nc.vector.tensor_copy(a5[:], a_win[t % 2][:].indirect(n5_t[:]))
+            s46 = work.tile([P, S], F32, name="s46")
+            nc.vector.tensor_tensor(s46[:], b_win[t % 2][:].indirect(n6_t[:]), a4[:], ADD)
+            s57 = work.tile([P, S], F32, name="s57")
+            nc.vector.tensor_tensor(s57[:], b_win[t % 2][:].indirect(n7_t[:]), a5[:], ADD)
+            best = work.tile([P, S], F32, name="best")
+            nc.vector.tensor_tensor(best[:], s46[:], s57[:], MAX)
+            nc.sync.dma_start(out_rows[t], best[:])

@@ -19,6 +19,7 @@ MAX = mybir.AluOpType.max
 
 P = 128
 PACK = 4
+W_PIECES = ((0, 256), (256, 256))
 Z_CHUNKS = ((0, 256), (256, 128), (384, 128))
 
 
@@ -41,20 +42,18 @@ def tile_picked_ccmppathbfoldd_none_p_kernel(tc, x_words, x_scales, w1, gs, offs
             nc.sync.dma_start(xs[32 * q : 32 * q + 4, :].bitcast(I32), x_scales[0, 4 * q : 4 * q + 4, :].bitcast(I32))
         offs_t = load_list("offs_t", offs)
         w_rows = w1.rearrange("(p j) c -> p j c", j=PACK)
-        w_raw = []
-        for half in range(2):
-            raw = keep.tile([P, PACK, H // 2], F32, name="w_raw%d" % half)
-            nc.sync.dma_start(raw[:], w_rows[:, :, half * (H // 2) : (half + 1) * (H // 2)])
-            w_raw.append(raw)
+        w_raw = [keep.tile([P, PACK, H // 2], F32, name="w_raw%d" % i) for i in range(2)]
+        nc.sync.dma_start(w_raw[0][:], w_rows[:, :, : H // 2])
+        ca_t = load_list("ca_t", ca)
+        nc.sync.dma_start(w_raw[1][:], w_rows[:, :, H // 2 :])
         xw = keep.tile([P, T], U32, name="xw", align_bytes=64)
         nc.sync.dma_start(xw[:].bitcast(I32), x_words[0].rearrange("p n t -> p (n t)").bitcast(I32))
-        ca_t = load_list("ca_t", ca)
-        cb_t = load_list("cb_t", cb)
         gs_t = keep.tile([P, PACK], F32, name="gs_t")
         nc.sync.dma_start(gs_t[:], gs.rearrange("(p t) o -> p (t o)", t=PACK))
         n1_t = load_list("n1_t", n1)
         n2_t = load_list("n2_t", n2)
         n3_t = load_list("n3_t", n3)
+        cb_t = load_list("cb_t", cb)
         n4_t = load_list("n4_t", n4)
         n5_t = load_list("n5_t", n5)
         n6_t = load_list("n6_t", n6)
@@ -85,27 +84,32 @@ def tile_picked_ccmppathbfoldd_none_p_kernel(tc, x_words, x_scales, w1, gs, offs
         ca_s = deal_bytes("ca_s", gather_bytes("ca_plain", ca_t))
 
         w_bf = keep.tile([P, PACK, P, PACK], BF16, name="w_bf", align_bytes=64)
-        for half in range(2):
+        for i, (c0, width) in enumerate(W_PIECES):
             nc.scalar.copy(
-                w_bf[:, :, half * 64 : (half + 1) * 64, :].rearrange("p t m j -> p m t j"),
-                w_raw[half][:].rearrange("p j (m t) -> p m t j", t=PACK),
+                w_bf[:, :, c0 // PACK : (c0 + width) // PACK, :].rearrange("p t m j -> p m t j"),
+                w_raw[i][:].rearrange("p j (m t) -> p m t j", t=PACK),
             )
         w_q = keep.tile([P, H], U32, name="w_q", align_bytes=64)
         w_s = keep.tile([P, H], U8, name="w_s", align_bytes=64)
         nc.vector.quantize_mx(out=w_q[:].bitcast(FP8X4), scales=w_s[:], in_=w_bf[:].rearrange("p t m j -> p (t m j)"))
 
         xq_w = keep.tile([P, S], U32, name="xq_w", align_bytes=64)
-        nc.vector.tensor_copy(xq_w[:], xw[:].indirect(offs_t[:]))
-
+        for c0 in range(0, S, S // 2):
+            nc.vector.tensor_copy(xq_w[:, c0 : c0 + S // 2], xw[:].indirect(offs_t[:, c0 // 16 : (c0 + S // 2) // 16]))
         banks = [psum.tile([P, S], F32, name="bank%d" % i) for i in range(8)]
-        ds = []
-        for t in range(PACK):
+        ds = [keep.tile([P, S], F32, name="ds%d" % t) for t in range(PACK)]
+
+        def project(t, bank, c0, width):
             cols = slice(t * P, (t + 1) * P)
-            nc.tensor.matmul_mx(banks[t][:], lhsT=w_q[:, cols].bitcast(FP8X4), lhsT_scale=w_s[:, cols],
-                                rhs=xq_w[:].bitcast(FP8X4), rhs_scale=xq_s[:], start=True, stop=True)
-            y = keep.tile([P, S], F32, name="ds%d" % t)
-            nc.scalar.activation(y[:], banks[t][:], COPY, scale=gs_t[:, t : t + 1])
-            ds.append(y)
+            picked = slice(c0, c0 + width)
+            nc.tensor.matmul_mx(bank[:, picked], lhsT=w_q[:, cols].bitcast(FP8X4), lhsT_scale=w_s[:, cols],
+                                rhs=xq_w[:, picked].bitcast(FP8X4), rhs_scale=xq_s[:, picked], start=True, stop=True)
+            nc.scalar.activation(ds[t][:, picked], bank[:, picked], COPY, scale=gs_t[:, t : t + 1])
+
+        project(0, banks[4], 0, S // 2)
+        project(0, banks[0], S // 2, S // 2)
+        for t in range(1, PACK):
+            project(t, banks[t], 0, S)
 
         ca_w = keep.tile([P, C], U32, name="ca_w", align_bytes=64)
         gather_dealt_words(ca_w, ca_t)
@@ -151,6 +155,13 @@ def tile_picked_ccmppathbfoldd_none_p_kernel(tc, x_words, x_scales, w1, gs, offs
         cb_s = deal_bytes("cb_s", cb_plain)
 
         out_rows = out.rearrange("(g t r) j -> t g r j", t=PACK, r=8)
+        sums = []
+
+        def finish(t, c0, width):
+            best = work.tile([P, width], F32, name="best")
+            nc.vector.tensor_tensor(best[:], sums[t][0][:, c0 : c0 + width], sums[t][1][:, c0 : c0 + width], MAX)
+            nc.sync.dma_start(out_rows[t][:, :, c0 : c0 + width], best[:])
+
         for t in range(PACK):
             cols = slice(t * P, (t + 1) * P)
             for words, scales, win, bank in ((ca_w, ca_s, a_win[t % 2], banks[2 * t]), (cb_w, cb_s, b_win[t % 2], banks[2 * t + 1])):
@@ -159,12 +170,14 @@ def tile_picked_ccmppathbfoldd_none_p_kernel(tc, x_words, x_scales, w1, gs, offs
                 nc.scalar.activation(win[:, :S], bank[:], COPY, scale=0.0625)
             a4 = work.tile([P, S], F32, name="a4")
             nc.vector.tensor_copy(a4[:], a_win[t % 2][:].indirect(n4_t[:]))
+            if t > 0:
+                finish(t - 1, 0, S)
             a5 = work.tile([P, S], F32, name="a5")
             nc.vector.tensor_copy(a5[:], a_win[t % 2][:].indirect(n5_t[:]))
             s46 = work.tile([P, S], F32, name="s46")
             nc.vector.tensor_tensor(s46[:], b_win[t % 2][:].indirect(n6_t[:]), a4[:], ADD)
             s57 = work.tile([P, S], F32, name="s57")
             nc.vector.tensor_tensor(s57[:], b_win[t % 2][:].indirect(n7_t[:]), a5[:], ADD)
-            best = work.tile([P, S], F32, name="best")
-            nc.vector.tensor_tensor(best[:], s46[:], s57[:], MAX)
-            nc.sync.dma_start(out_rows[t], best[:])
+            sums.append((s46, s57))
+        finish(PACK - 1, 0, S // 2)
+        finish(PACK - 1, S // 2, S // 2)

@@ -1,6 +1,7 @@
 from contextlib import ExitStack
 
 import concourse.mybir as mybir
+from concourse.masks import make_identity
 
 K, T, S, H, W, C = 512, 2048, 512, 512, 256, 512
 FLOPS = 2 * K * H * S + 2 * 2 * K * C * S
@@ -15,6 +16,8 @@ FP8X4 = mybir.dt.float8_e4m3fn_x4
 COPY = mybir.ActivationFunctionType.Copy
 ADD = mybir.AluOpType.add
 MULT = mybir.AluOpType.mult
+RELU = mybir.ActivationFunctionType.Relu
+SUB = mybir.AluOpType.subtract
 MAX = mybir.AluOpType.max
 
 P = 128
@@ -63,6 +66,9 @@ def tile_picked_ccmppathbfoldd_none_p_kernel(tc, x_words, x_scales, w1, gs, offs
         b_win = [keep.tile([P, 2 * S], F32, name="b_win%d" % t) for t in range(2)]
         for win in a_win + b_win:
             nc.vector.memset(win[:, S:], 0.0)
+
+        ident = keep.tile([P, P], F32, name="ident")
+        make_identity(nc, ident[:])
 
         def gather_bytes(name, lst):
             tile = keep.tile([P, S], U8, name=name, align_bytes=64)
@@ -155,29 +161,60 @@ def tile_picked_ccmppathbfoldd_none_p_kernel(tc, x_words, x_scales, w1, gs, offs
         cb_s = deal_bytes("cb_s", cb_plain)
 
         out_rows = out.rearrange("(g t r) j -> t g r j", t=PACK, r=8)
-        sums = []
+        score_banks = banks[:5]
+        diff_bank, first_bank, out_bank = banks[5:]
 
-        def finish(t, c0, width):
-            best = work.tile([P, width], F32, name="best")
-            nc.vector.tensor_tensor(best[:], sums[t][0][:, c0 : c0 + width], sums[t][1][:, c0 : c0 + width], MAX)
-            nc.sync.dma_start(out_rows[t][:, :, c0 : c0 + width], best[:])
-
-        for t in range(PACK):
+        def score(t):
             cols = slice(t * P, (t + 1) * P)
-            for words, scales, win, bank in ((ca_w, ca_s, a_win[t % 2], banks[2 * t]), (cb_w, cb_s, b_win[t % 2], banks[2 * t + 1])):
+            for i, (words, scales, win, factor) in enumerate(
+                ((ca_w, ca_s, a_win[t % 2], 0.0625), (cb_w, cb_s, b_win[t % 2], -0.0625))
+            ):
+                bank = score_banks[(2 * t + i) % len(score_banks)]
                 nc.tensor.matmul_mx(bank[:], lhsT=words[:, cols].bitcast(FP8X4), lhsT_scale=scales[:, cols],
                                     rhs=z_q[:].bitcast(FP8X4), rhs_scale=z_s[:], start=True, stop=True)
-                nc.scalar.activation(win[:, :S], bank[:], COPY, scale=0.0625)
-            a4 = work.tile([P, S], F32, name="a4")
-            nc.vector.tensor_copy(a4[:], a_win[t % 2][:].indirect(n4_t[:]))
-            if t > 0:
-                finish(t - 1, 0, S)
+                nc.scalar.activation(win[:, :S], bank[:], COPY, scale=factor)
+
+        def turn_and_add(bank, terms):
+            for i, term in enumerate(terms):
+                for c0 in range(0, S, P):
+                    nc.tensor.matmul(bank[:, c0 : c0 + P], lhsT=term[:, c0 : c0 + P], rhs=ident[:], is_transpose=True,
+                                     start=(i == 0 and c0 == 0), stop=(i == len(terms) - 1 and c0 == S - P))
+
+        def fetch_a5(t):
             a5 = work.tile([P, S], F32, name="a5")
             nc.vector.tensor_copy(a5[:], a_win[t % 2][:].indirect(n5_t[:]))
-            s46 = work.tile([P, S], F32, name="s46")
-            nc.vector.tensor_tensor(s46[:], b_win[t % 2][:].indirect(n6_t[:]), a4[:], ADD)
-            s57 = work.tile([P, S], F32, name="s57")
-            nc.vector.tensor_tensor(s57[:], b_win[t % 2][:].indirect(n7_t[:]), a5[:], ADD)
-            sums.append((s46, s57))
-        finish(PACK - 1, 0, S // 2)
-        finish(PACK - 1, S // 2, S // 2)
+            return a5
+
+        score(0)
+        score(1)
+        a5s = [fetch_a5(0), fetch_a5(1)]
+        for t in range(PACK):
+            if t >= 2:
+                score(t)
+                a5s.append(fetch_a5(t))
+            nb6 = work.tile([P, S], F32, name="nb6")
+            nc.vector.tensor_copy(nb6[:], b_win[t % 2][:].indirect(n6_t[:]))
+            neg_second = work.tile([P, S], F32, name="neg_second")
+            nc.vector.tensor_tensor(neg_second[:], b_win[t % 2][:].indirect(n7_t[:]), a5s[t][:], SUB)
+            first = work.tile([P, S], F32, name="first")
+            if t < PACK - 1:
+                nc.vector.tensor_tensor(first[:], a_win[t % 2][:].indirect(n4_t[:]), nb6[:], SUB)
+                turn_and_add(diff_bank, (neg_second, first))
+                excess = work.tile([P, S], F32, name="excess")
+                nc.scalar.activation(excess[:], diff_bank[:], RELU, scale=-1.0)
+                turn_and_add(first_bank, (first,))
+                first_turned = work.tile([P, S], F32, name="first_turned")
+                nc.scalar.copy(first_turned[:], first_bank[:])
+                turn_and_add(out_bank, (excess, first_turned))
+                best = work.tile([P, S], F32, name="best")
+                nc.scalar.copy(best[:], out_bank[:])
+                nc.scalar.dma_start(out_rows[t], best[:])
+            else:
+                halves_of_s = [slice(0, S // 2), slice(S // 2, S)]
+                for cols in halves_of_s:
+                    nc.vector.tensor_tensor(first[:, cols], a_win[t % 2][:].indirect(n4_t[:, cols.start // 16 : cols.stop // 16]),
+                                            nb6[:, cols], SUB)
+                for cols in halves_of_s:
+                    last = work.tile([P, S // 2], F32, name="last")
+                    nc.vector.scalar_tensor_tensor(last[:], neg_second[:, cols], -1.0, first[:, cols], MULT, MAX)
+                    nc.sync.dma_start(out_rows[t][:, :, cols], last[:])

from contextlib import ExitStack

import concourse.mybir as mybir
from concourse.masks import make_identity

K, T, S, H, W, C = 512, 2048, 512, 512, 256, 512
FLOPS = 2 * K * H * S + 2 * 2 * K * C * S

F32 = mybir.dt.float32
BF16 = mybir.dt.bfloat16
I32 = mybir.dt.int32
U32 = mybir.dt.uint32
U16 = mybir.dt.uint16
U8 = mybir.dt.uint8
FP8X4 = mybir.dt.float8_e4m3fn_x4
COPY = mybir.ActivationFunctionType.Copy
ADD = mybir.AluOpType.add
MULT = mybir.AluOpType.mult
RELU = mybir.ActivationFunctionType.Relu
SUB = mybir.AluOpType.subtract
MAX = mybir.AluOpType.max

P = 128
PACK = 4
W_PIECES = ((0, 256), (256, 256))
Z_CHUNKS = ((0, 256), (256, 128), (384, 128))


def tile_picked_ccmppathbfoldd_none_p_kernel(tc, x_words, x_scales, w1, gs, offs, n1, n2, n3, ca, cb, n4, n5, n6, n7, out):
    nc = tc.nc
    with ExitStack() as ctx:
        lists = ctx.enter_context(tc.tile_pool(name="lists", bufs=1))
        keep = ctx.enter_context(tc.tile_pool(name="keep", bufs=1))
        work = ctx.enter_context(tc.tile_pool(name="work", bufs=2))
        psum = ctx.enter_context(tc.psum_pool(name="psum", bufs=1))

        def load_list(name, src):
            tile = lists.tile(list(src.shape), U16, name=name)
            nc.sync.dma_start(tile[:], src)
            return tile

        xs = keep.tile([P, T], U8, name="xs", align_bytes=64)
        nc.vector.memset(xs[:].bitcast(I32), 0)
        for q in range(4):
            nc.sync.dma_start(xs[32 * q : 32 * q + 4, :].bitcast(I32), x_scales[0, 4 * q : 4 * q + 4, :].bitcast(I32))
        offs_t = load_list("offs_t", offs)
        w_rows = w1.rearrange("(p j) c -> p j c", j=PACK)
        w_raw = [keep.tile([P, PACK, H // 2], F32, name="w_raw%d" % i) for i in range(2)]
        nc.sync.dma_start(w_raw[0][:], w_rows[:, :, : H // 2])
        ca_t = load_list("ca_t", ca)
        nc.sync.dma_start(w_raw[1][:], w_rows[:, :, H // 2 :])
        xw = keep.tile([P, T], U32, name="xw", align_bytes=64)
        nc.sync.dma_start(xw[:].bitcast(I32), x_words[0].rearrange("p n t -> p (n t)").bitcast(I32))
        gs_t = keep.tile([P, PACK], F32, name="gs_t")
        nc.sync.dma_start(gs_t[:], gs.rearrange("(p t) o -> p (t o)", t=PACK))
        n1_t = load_list("n1_t", n1)
        n2_t = load_list("n2_t", n2)
        n3_t = load_list("n3_t", n3)
        cb_t = load_list("cb_t", cb)
        n4_t = load_list("n4_t", n4)
        n5_t = load_list("n5_t", n5)
        n6_t = load_list("n6_t", n6)
        n7_t = load_list("n7_t", n7)

        a_win = [keep.tile([P, 2 * S], F32, name="a_win%d" % t) for t in range(2)]
        b_win = [keep.tile([P, 2 * S], F32, name="b_win%d" % t) for t in range(2)]
        for win in a_win + b_win:
            nc.vector.memset(win[:, S:], 0.0)

        ident = keep.tile([P, P], F32, name="ident")
        make_identity(nc, ident[:])

        def gather_bytes(name, lst):
            tile = keep.tile([P, S], U8, name=name, align_bytes=64)
            nc.vector.tensor_copy(tile[:], xs[:].indirect(lst[:]))
            return tile

        def deal_bytes(name, plain):
            tile = keep.tile([P, S], U8, name=name, align_bytes=64)
            nc.vector.tensor_copy(
                tile[:].bitcast(I32).rearrange("p (t g r) -> p t g r", t=PACK, r=2),
                plain[:].bitcast(I32).rearrange("p (g t r) -> p t g r", t=PACK, r=2),
            )
            return tile

        def gather_dealt_words(tile, lst):
            nc.vector.tensor_copy(tile[:].rearrange("p (t g r) -> p g t r", t=PACK, r=8), xw[:].indirect(lst[:]))

        xq_s = gather_bytes("xq_s", offs_t)
        ca_s = deal_bytes("ca_s", gather_bytes("ca_plain", ca_t))

        w_bf = keep.tile([P, PACK, P, PACK], BF16, name="w_bf", align_bytes=64)
        for i, (c0, width) in enumerate(W_PIECES):
            nc.scalar.copy(
                w_bf[:, :, c0 // PACK : (c0 + width) // PACK, :].rearrange("p t m j -> p m t j"),
                w_raw[i][:].rearrange("p j (m t) -> p m t j", t=PACK),
            )
        w_q = keep.tile([P, H], U32, name="w_q", align_bytes=64)
        w_s = keep.tile([P, H], U8, name="w_s", align_bytes=64)
        nc.vector.quantize_mx(out=w_q[:].bitcast(FP8X4), scales=w_s[:], in_=w_bf[:].rearrange("p t m j -> p (t m j)"))

        xq_w = keep.tile([P, S], U32, name="xq_w", align_bytes=64)
        for c0 in range(0, S, S // 2):
            nc.vector.tensor_copy(xq_w[:, c0 : c0 + S // 2], xw[:].indirect(offs_t[:, c0 // 16 : (c0 + S // 2) // 16]))
        banks = [psum.tile([P, S], F32, name="bank%d" % i) for i in range(8)]
        ds = [keep.tile([P, S], F32, name="ds%d" % t) for t in range(PACK)]

        def project(t, bank, c0, width):
            cols = slice(t * P, (t + 1) * P)
            picked = slice(c0, c0 + width)
            nc.tensor.matmul_mx(bank[:, picked], lhsT=w_q[:, cols].bitcast(FP8X4), lhsT_scale=w_s[:, cols],
                                rhs=xq_w[:, picked].bitcast(FP8X4), rhs_scale=xq_s[:, picked], start=True, stop=True)
            nc.scalar.activation(ds[t][:, picked], bank[:, picked], COPY, scale=gs_t[:, t : t + 1])

        project(0, banks[4], 0, S // 2)
        project(0, banks[0], S // 2, S // 2)
        for t in range(1, PACK):
            project(t, banks[t], 0, S)

        ca_w = keep.tile([P, C], U32, name="ca_w", align_bytes=64)
        gather_dealt_words(ca_w, ca_t)

        halves = []
        pa = []
        pb = []
        for t in range(PACK + 1):
            if t < PACK:
                first = keep.tile([P, W], F32, name="pa%d" % t)
                nc.vector.tensor_copy(first[:], ds[t][:].indirect(n1_t[:]))
                second = keep.tile([P, W], F32, name="pb%d" % t)
                nc.vector.tensor_scalar(second[:], ds[t][:].indirect(n2_t[:]), -0.5, 0.0, MULT, ADD)
                pa.append(first)
                pb.append(second)
            if t > 0:
                u = t - 1
                nc.vector.tensor_tensor(ds[u][:].indirect(n2_t[:]), pa[u][:], pb[u][:], ADD)
                half_ds = keep.tile([P, S], F32, name="half_ds%d" % u, tag="half_ds%d" % u, align_bytes=64)
                nc.scalar.activation(half_ds[:], ds[u][:], COPY, scale=-0.5)
                halves.append(half_ds)

        z_q = keep.tile([P, S], U32, name="z_q", align_bytes=64)
        z_s = keep.tile([P, S], U8, name="z_s", align_bytes=64)
        z_bf = []
        for i, (c0, width) in enumerate(Z_CHUNKS):
            zf = keep.tile([P, PACK, width], F32, name="zf%d" % i)
            for t in range(PACK):
                nc.vector.tensor_tensor(zf[:, t, :], halves[t][:].indirect(n3_t[:, c0 // 16 : (c0 + width) // 16]),
                                        ds[t][:, c0 : c0 + width], ADD)
            zb = keep.tile([P, width, PACK], BF16, name="zb%d" % i, tag="zb%d" % i, align_bytes=64)
            nc.scalar.copy(zb[:], zf[:].rearrange("p t c -> p c t"))
            z_bf.append(zb)
            if i == len(Z_CHUNKS) - 1:
                cb_w = keep.tile([P, C], U32, name="cb_w", tag="half_ds3", align_bytes=64)
                gather_dealt_words(cb_w, cb_t)
            for j in ([i - 1] if i > 0 else []) + ([i] if i == len(Z_CHUNKS) - 1 else []):
                d0, dw = Z_CHUNKS[j]
                nc.vector.quantize_mx(out=z_q[:, d0 : d0 + dw].bitcast(FP8X4), scales=z_s[:, d0 : d0 + dw],
                                      in_=z_bf[j][:].rearrange("p c t -> p (c t)"))
        cb_plain = keep.tile([P, S], U8, name="cb_plain", tag="zb2", align_bytes=64)
        nc.vector.tensor_copy(cb_plain[:], xs[:].indirect(cb_t[:]))
        cb_s = deal_bytes("cb_s", cb_plain)

        out_rows = out.rearrange("(g t r) j -> t g r j", t=PACK, r=8)
        score_banks = banks[:5]
        diff_bank, first_bank, out_bank = banks[5:]

        def score(t):
            cols = slice(t * P, (t + 1) * P)
            for i, (words, scales, win, factor) in enumerate(
                ((ca_w, ca_s, a_win[t % 2], 0.0625), (cb_w, cb_s, b_win[t % 2], -0.0625))
            ):
                bank = score_banks[(2 * t + i) % len(score_banks)]
                nc.tensor.matmul_mx(bank[:], lhsT=words[:, cols].bitcast(FP8X4), lhsT_scale=scales[:, cols],
                                    rhs=z_q[:].bitcast(FP8X4), rhs_scale=z_s[:], start=True, stop=True)
                nc.scalar.activation(win[:, :S], bank[:], COPY, scale=factor)

        def turn_and_add(bank, terms):
            for i, term in enumerate(terms):
                for c0 in range(0, S, P):
                    nc.tensor.matmul(bank[:, c0 : c0 + P], lhsT=term[:, c0 : c0 + P], rhs=ident[:], is_transpose=True,
                                     start=(i == 0 and c0 == 0), stop=(i == len(terms) - 1 and c0 == S - P))

        def fetch_a5(t):
            a5 = work.tile([P, S], F32, name="a5")
            nc.vector.tensor_copy(a5[:], a_win[t % 2][:].indirect(n5_t[:]))
            return a5

        score(0)
        score(1)
        a5s = [fetch_a5(0), fetch_a5(1)]
        for t in range(PACK):
            if t >= 2:
                score(t)
                a5s.append(fetch_a5(t))
            nb6 = work.tile([P, S], F32, name="nb6")
            nc.vector.tensor_copy(nb6[:], b_win[t % 2][:].indirect(n6_t[:]))
            neg_second = work.tile([P, S], F32, name="neg_second")
            nc.vector.tensor_tensor(neg_second[:], b_win[t % 2][:].indirect(n7_t[:]), a5s[t][:], SUB)
            first = work.tile([P, S], F32, name="first")
            if t < PACK - 1:
                nc.vector.tensor_tensor(first[:], a_win[t % 2][:].indirect(n4_t[:]), nb6[:], SUB)
                turn_and_add(diff_bank, (neg_second, first))
                excess = work.tile([P, S], F32, name="excess")
                nc.scalar.activation(excess[:], diff_bank[:], RELU, scale=-1.0)
                turn_and_add(first_bank, (first,))
                first_turned = work.tile([P, S], F32, name="first_turned")
                nc.scalar.copy(first_turned[:], first_bank[:])
                turn_and_add(out_bank, (excess, first_turned))
                best = work.tile([P, S], F32, name="best")
                nc.scalar.copy(best[:], out_bank[:])
                nc.scalar.dma_start(out_rows[t], best[:])
            else:
                halves_of_s = [slice(0, S // 2), slice(S // 2, S)]
                for cols in halves_of_s:
                    nc.vector.tensor_tensor(first[:, cols], a_win[t % 2][:].indirect(n4_t[:, cols.start // 16 : cols.stop // 16]),
                                            nb6[:, cols], SUB)
                for cols in halves_of_s:
                    last = work.tile([P, S // 2], F32, name="last")
                    nc.vector.scalar_tensor_tensor(last[:], neg_second[:, cols], -1.0, first[:, cols], MULT, MAX)
                    nc.sync.dma_start(out_rows[t][:, :, cols], last[:])
